import numpy as np
import ml_dtypes


def mxq(x, axis, fmt="e4m3"):
    dtype, down = {"e4m3": (ml_dtypes.float8_e4m3fn, 7), "e5m2": (ml_dtypes.float8_e5m2, 14)}[fmt]
    v = np.moveaxis(np.asarray(x, np.float32).astype(ml_dtypes.bfloat16).astype(np.float64), axis, -1)
    blocks = v.reshape(v.shape[:-1] + (-1, 32))
    amax = np.abs(blocks).max(-1, keepdims=True)
    byte = np.maximum(np.where(amax > 0, np.frexp(amax)[1] - 1 + 127, 0) - down, 1)
    scale = np.exp2(byte - 127.0)
    codes = (blocks / scale).astype(np.float32).astype(dtype).astype(np.float64)
    return np.moveaxis((codes * scale).reshape(v.shape), -1, axis)


WIDE = False


def mx_kscale(k):
    if not WIDE:
        return np.ones(k)
    levels = np.array([10, -10, 5, -5, 0])
    if k % 512:
        return np.exp2(np.random.permutation(np.resize(levels, k // 32))).repeat(32)
    a = np.empty((k // 512, 16))
    for p in range(k // 512):
        a[p, :8] = np.random.permutation(np.resize(levels, 8))
        for g in range(8):
            far = levels[np.abs(levels - a[p, g]) >= 10]
            a[p, g + 8] = far[np.random.randint(len(far))]
    return np.exp2(a.ravel()).repeat(32)


def f64(x):
    return np.asarray(x).astype(np.float64)


def striped(idx):
    return np.tile(np.asarray(idx).reshape(-1, 16).T, (8, 1)).astype(np.uint16)


def unstriped(offs):
    return offs[:16].T.reshape(-1).astype(np.int64)


N, T, D, H, M, G, K = 512, 2048, 512, 512, 128, 1024, 1


def setup_inputs():
    n = np.random.standard_normal
    s = mx_kscale(D)[:, None]
    u = mx_kscale(H)[:, None]
    return {
        "xT": (n((D, T)) * s).astype(np.float32),
        "w1": (n((D, H)) / np.sqrt(D) / s * u[:, 0]).astype(np.float32),
        "w2": (n((H, M)) / np.sqrt(H * K) / u).astype(np.float32),
        "offs": striped(np.random.permutation(T)[:N]),
        "offs2": striped(np.random.randint(0, N, G * K)),
    }


def reference(xT, w1, w2, offs, offs2):
    a = mxq(f64(w1), 0, "e4m3").T @ mxq(f64(xT)[:, unstriped(offs)], 0, "e4m3")
    h = np.maximum(a, 0.0)
    e = h[:, unstriped(offs2)].reshape(H, G, K).sum(-1)
    return mxq(f64(w2), 0, "e4m3").T @ mxq(e, 0, "e4m3")

@@ -1,0 +1,185 @@
+import concourse.mybir as mybir
+
+D, T, N, H, M, G = 512, 2048, 512, 512, 128, 1024
+FLOPS = 2 * D * H * N + 2 * H * M * G
+
+F32 = mybir.dt.float32
+BF16 = mybir.dt.bfloat16
+U32 = mybir.dt.uint32
+U16 = mybir.dt.uint16
+U8 = mybir.dt.uint8
+FP8X4 = mybir.dt.float8_e4m3fn_x4
+COPY = mybir.ActivationFunctionType.Copy
+RELU = mybir.ActivationFunctionType.Relu
+
+P = 128
+PACK = 4
+W1_CUTS = ((0, 256), (256, 512))
+WINDOW = 544
+PIECES = (512, 256, 128, 128)
+
+
+def tile_attend_hop_pick_kernel(tc, xT, w1, w2, offs, offs2, out):
+    nc = tc.nc
+    with (
+        tc.tile_pool(name="held", bufs=1) as held,
+        tc.psum_pool(name="psum", bufs=1) as psum,
+    ):
+        list1 = held.tile([P, N // 16], U16, name="list1")
+        list2 = held.tile([P, G // 16], U16, name="list2")
+        xp = [held.tile([P, T], F32, name=f"xp{t}", align_bytes=64) for t in range(PACK)]
+        w1raw = [held.tile([P, PACK, hi - lo], F32, name=f"w1raw{k}", align_bytes=64) for k, (lo, hi) in enumerate(W1_CUTS)]
+        w2raw = held.tile([P, PACK, M], F32, name="w2raw", align_bytes=64)
+        xb = held.tile([P, N, PACK], BF16, name="xb", align_bytes=64)
+        xq = held.tile([P, N], U32, name="xq", align_bytes=64)
+        xs = held.tile([P, N], U8, name="xs", align_bytes=64)
+        w1b = held.tile([P, PACK, P, PACK], BF16, name="w1b", align_bytes=64)
+        w1q = held.tile([P, PACK, P], U32, name="w1q", align_bytes=64)
+        w1s = held.tile([P, PACK, P], U8, name="w1s", align_bytes=64)
+        w2b = held.tile([P, M, PACK], BF16, name="w2b", align_bytes=64)
+        w2q = held.tile([P, M], U32, name="w2q", align_bytes=64)
+        w2s = held.tile([P, M], U8, name="w2s", align_bytes=64)
+        h = [held.tile([P, WINDOW], F32, name=f"h{t}", align_bytes=64) for t in range(PACK)]
+        ef = [held.tile([P, PACK, n], F32, name=f"ef{k}", align_bytes=64) for k, n in enumerate(PIECES)]
+        eb = [held.tile([P, n, PACK], BF16, name=f"eb{k}", align_bytes=64) for k, n in enumerate(PIECES)]
+        eq = [held.tile([P, n], U32, name=f"eq{k}", align_bytes=64) for k, n in enumerate(PIECES)]
+        es = [held.tile([P, n], U8, name=f"es{k}", align_bytes=64) for k, n in enumerate(PIECES)]
+        res = [held.tile([P, n], F32, name=f"res{k}", align_bytes=64) for k, n in enumerate(PIECES)]
+
+        x_rows = xT.rearrange("(p t) n -> p t n", t=PACK)
+        w1_rows = w1.rearrange("(p j) c -> p j c", j=PACK)
+        w2_rows = w2.rearrange("(p j) m -> p j m", j=PACK)
+        nc.sync.dma_start(list1[:], offs)
+        nc.sync.dma_start(list2[:], offs2)
+        for t in range(3):
+            nc.sync.dma_start(xp[t][:], x_rows[:, t, :])
+        nc.sync.dma_start(w1raw[0][:], w1_rows[:, :, slice(*W1_CUTS[0])])
+        nc.sync.dma_start(xp[3][:], x_rows[:, 3, :])
+        nc.sync.dma_start(w1raw[1][:], w1_rows[:, :, slice(*W1_CUTS[1])])
+        nc.sync.dma_start(w2raw[:], w2_rows)
+        for t in range(PACK):
+            nc.gpsimd.memset(h[t][:, N:WINDOW], 0.0)
+
+        def w1_slice(k, t0, t1):
+            lo, hi = W1_CUTS[k]
+            m0, m1 = lo // PACK, hi // PACK
+            src = w1raw[k][:].rearrange("p j (m t) -> p m t j", t=PACK)
+            dst = w1b[:].rearrange("p t m j -> p m t j")
+            nc.scalar.activation(dst[:, m0:m1, t0:t1, :], src[:, :, t0:t1, :], COPY)
+
+        def quantize_w1(t):
+            nc.vector.quantize_mx(
+                out=w1q[:, t, :].bitcast(FP8X4),
+                scales=w1s[:, t, :],
+                in_=w1b[:, t, :, :].rearrange("p m j -> p (m j)"),
+            )
+
+        for t in range(3):
+            nc.vector.tensor_copy(xb[:, :, t], xp[t][:].indirect(list1[:]))
+        w1_slice(0, 0, PACK)
+        half = N // 2
+        for a in range(2):
+            nc.vector.tensor_copy(
+                xb[:, a * half : (a + 1) * half, 3],
+                xp[3][:].indirect(list1[:, a * half // 16 : (a + 1) * half // 16]),
+            )
+
+        for t in range(2):
+            w1_slice(1, t, t + 1)
+
+        def quantize_x(a):
+            cols = slice(a * half, (a + 1) * half)
+            nc.vector.quantize_mx(
+                out=xq[:, cols].bitcast(FP8X4),
+                scales=xs[:, cols],
+                in_=xb[:, cols, :].rearrange("p n j -> p (n j)"),
+            )
+
+        def first_product(bank, t, cols):
+            nc.tensor.matmul_mx(
+                out=bank,
+                lhsT=w1q[:, t, :].bitcast(FP8X4),
+                lhsT_scale=w1s[:, t, :],
+                rhs=xq[:, cols].bitcast(FP8X4),
+                rhs_scale=xs[:, cols],
+                start=True,
+                stop=True,
+            )
+
+        quantize_x(0)
+        quantize_w1(0)
+        quantize_x(1)
+        bank0 = [psum.tile([P, half], F32, name=f"bank0{a}") for a in range(2)]
+        for a in range(2):
+            first_product(bank0[a][:], 0, slice(a * half, (a + 1) * half))
+        nc.scalar.activation(h[0][:, :half], bank0[0][:], RELU)
+        nc.vector.tensor_relu(h[0][:, half:N], bank0[1][:])
+
+        starts = [sum(PIECES[:k]) for k in range(len(PIECES))]
+
+        def gather(k, t):
+            lo, hi = starts[k], starts[k] + PIECES[k]
+            nc.vector.tensor_copy(ef[k][:, t, :], h[t][:].indirect(list2[:, lo // 16 : hi // 16]))
+
+        def quantize_e(k):
+            nc.vector.quantize_mx(
+                out=eq[k][:].bitcast(FP8X4),
+                scales=es[k][:],
+                in_=eb[k][:].rearrange("p n j -> p (n j)"),
+            )
+
+        def interleave(k):
+            nc.scalar.activation(eb[k][:], ef[k][:].rearrange("p t n -> p n t"), COPY)
+
+        obank = [psum.tile([P, n], F32, name=f"obank{k}", tag=f"ob{min(k, 2)}") for k, n in enumerate(PIECES[:3])]
+
+        def second_product(k, bank):
+            nc.tensor.matmul_mx(
+                out=bank,
+                lhsT=w2q[:].bitcast(FP8X4),
+                lhsT_scale=w2s[:],
+                rhs=eq[k][:].bitcast(FP8X4),
+                rhs_scale=es[k][:],
+                start=True,
+                stop=True,
+            )
+
+        def finish(k, bank):
+            nc.scalar.activation(res[k][:], bank, COPY)
+            nc.sync.dma_start(out[:, starts[k] : starts[k] + PIECES[k]], res[k][:])
+
+        for t in range(1, PACK):
+            if t > 1:
+                w1_slice(1, t, t + 1)
+            quantize_w1(t)
+            bank = psum.tile([P, N], F32, name=f"bank{t}")
+            first_product(bank[:], t, slice(0, N))
+            gather(0, t - 1)
+            nc.scalar.activation(h[t][:, :N], bank[:], RELU)
+        gather(0, PACK - 1)
+        nc.scalar.activation(w2b[:], w2raw[:].rearrange("p j m -> p m j"), COPY)
+        interleave(0)
+        for t in range(PACK):
+            gather(1, t)
+        nc.vector.quantize_mx(out=w2q[:].bitcast(FP8X4), scales=w2s[:], in_=w2b[:].rearrange("p m j -> p (m j)"))
+        quantize_e(0)
+        second_product(0, obank[0][:])
+        interleave(1)
+        for t in range(PACK):
+            gather(2, t)
+        finish(0, obank[0][:])
+        quantize_e(1)
+        second_product(1, obank[1][:])
+        interleave(2)
+        for t in range(PACK):
+            gather(3, t)
+        finish(1, obank[1][:])
+        nc.scalar.activation(eb[3][:, :, 0:2], ef[3][:, 0:2, :].rearrange("p t n -> p n t"), COPY)
+        quantize_e(2)
+        second_product(2, obank[2][:])
+        nc.vector.tensor_copy(eb[3][:, :, 2:4], ef[3][:, 2:4, :].rearrange("p t n -> p n t"))
+        finish(2, obank[2][:])
+        quantize_e(3)
+        last = psum.tile([P, PIECES[3]], F32, name="obank3", tag="ob0")
+        second_product(3, last[:])
+        finish(3, last[:])

@@ -15,7 +15,8 @@ RELU = mybir.ActivationFunctionType.Relu
 P = 128
 PACK = 4
 W1_CUTS = ((0, 256), (256, 512))
-WINDOW = 544
+CUT = 896
+WINDOWS = (912, 912, 912, 544)
 PIECES = (512, 256, 128, 128)
 
 
@@ -39,8 +40,8 @@ def tile_attend_hop_pick_kernel(tc, xT, w1, w2, offs, offs2, out):
         w2b = held.tile([P, M, PACK], BF16, name="w2b", align_bytes=64)
         w2q = held.tile([P, M], U32, name="w2q", align_bytes=64)
         w2s = held.tile([P, M], U8, name="w2s", align_bytes=64)
-        h = [held.tile([P, WINDOW], F32, name=f"h{t}", align_bytes=64) for t in range(PACK)]
-        ef = [held.tile([P, PACK, n], F32, name=f"ef{k}", align_bytes=64) for k, n in enumerate(PIECES)]
+        h = [held.tile([P, w], F32, name=f"h{t}", align_bytes=64) for t, w in enumerate(WINDOWS)]
+        ef = [held.tile([P, 2, G], F32, name=f"ef{k}", align_bytes=64) for k in range(2)]
         eb = [held.tile([P, n, PACK], BF16, name=f"eb{k}", align_bytes=64) for k, n in enumerate(PIECES)]
         eq = [held.tile([P, n], U32, name=f"eq{k}", align_bytes=64) for k, n in enumerate(PIECES)]
         es = [held.tile([P, n], U8, name=f"es{k}", align_bytes=64) for k, n in enumerate(PIECES)]
@@ -58,7 +59,7 @@ def tile_attend_hop_pick_kernel(tc, xT, w1, w2, offs, offs2, out):
         nc.sync.dma_start(w1raw[1][:], w1_rows[:, :, slice(*W1_CUTS[1])])
         nc.sync.dma_start(w2raw[:], w2_rows)
         for t in range(PACK):
-            nc.gpsimd.memset(h[t][:, N:WINDOW], 0.0)
+            nc.gpsimd.memset(h[t][:, N:], 0.0)
 
         def w1_slice(k, t0, t1):
             lo, hi = W1_CUTS[k]
@@ -84,8 +85,8 @@ def tile_attend_hop_pick_kernel(tc, xT, w1, w2, offs, offs2, out):
                 xp[3][:].indirect(list1[:, a * half // 16 : (a + 1) * half // 16]),
             )
 
-        for t in range(2):
-            w1_slice(1, t, t + 1)
+        w1_slice(1, 0, 1)
+        w1_slice(1, 1, PACK)
 
         def quantize_x(a):
             cols = slice(a * half, (a + 1) * half)
@@ -114,12 +115,28 @@ def tile_attend_hop_pick_kernel(tc, xT, w1, w2, offs, offs2, out):
             first_product(bank0[a][:], 0, slice(a * half, (a + 1) * half))
         nc.scalar.activation(h[0][:, :half], bank0[0][:], RELU)
         nc.vector.tensor_relu(h[0][:, half:N], bank0[1][:])
+        for t in range(1, PACK):
+            quantize_w1(t)
+            bank = psum.tile([P, N], F32, name=f"bank{t}")
+            first_product(bank[:], t, slice(0, N))
+            nc.scalar.activation(h[t][:, :N], bank[:], RELU)
+        nc.scalar.activation(w2b[:], w2raw[:].rearrange("p j m -> p m j"), COPY)
+        nc.vector.quantize_mx(out=w2q[:].bitcast(FP8X4), scales=w2s[:], in_=w2b[:].rearrange("p m j -> p (m j)"))
 
         starts = [sum(PIECES[:k]) for k in range(len(PIECES))]
 
-        def gather(k, t):
-            lo, hi = starts[k], starts[k] + PIECES[k]
-            nc.vector.tensor_copy(ef[k][:, t, :], h[t][:].indirect(list2[:, lo // 16 : hi // 16]))
+        def gather(t, lo, hi):
+            nc.vector.tensor_copy(ef[t // 2][:, t % 2, lo:hi], h[t][:].indirect(list2[:, lo // 16 : hi // 16]))
+
+        def pair(engine_copy, k, half_word):
+            cols = slice(starts[k], starts[k] + PIECES[k])
+            engine_copy(
+                eb[k][:, :, 2 * half_word : 2 * half_word + 2],
+                ef[half_word][:, :, cols].rearrange("p t n -> p n t"),
+            )
+
+        def scalar_copy(dst, src):
+            nc.scalar.activation(dst, src, COPY)
 
         def quantize_e(k):
             nc.vector.quantize_mx(
@@ -128,14 +145,10 @@ def tile_attend_hop_pick_kernel(tc, xT, w1, w2, offs, offs2, out):
                 in_=eb[k][:].rearrange("p n j -> p (n j)"),
             )
 
-        def interleave(k):
-            nc.scalar.activation(eb[k][:], ef[k][:].rearrange("p t n -> p n t"), COPY)
-
-        obank = [psum.tile([P, n], F32, name=f"obank{k}", tag=f"ob{min(k, 2)}") for k, n in enumerate(PIECES[:3])]
-
-        def second_product(k, bank):
+        def second_product(k):
+            bank = psum.tile([P, PIECES[k]], F32, name=f"obank{k}", tag="bank00" if k == 3 else f"ob{k}")
             nc.tensor.matmul_mx(
-                out=bank,
+                out=bank[:],
                 lhsT=w2q[:].bitcast(FP8X4),
                 lhsT_scale=w2s[:],
                 rhs=eq[k][:].bitcast(FP8X4),
@@ -143,43 +156,20 @@ def tile_attend_hop_pick_kernel(tc, xT, w1, w2, offs, offs2, out):
                 start=True,
                 stop=True,
             )
-
-        def finish(k, bank):
-            nc.scalar.activation(res[k][:], bank, COPY)
+            (nc.vector.tensor_copy if k > 2 else nc.scalar.copy)(res[k][:], bank[:])
             nc.sync.dma_start(out[:, starts[k] : starts[k] + PIECES[k]], res[k][:])
 
-        for t in range(1, PACK):
-            if t > 1:
-                w1_slice(1, t, t + 1)
-            quantize_w1(t)
-            bank = psum.tile([P, N], F32, name=f"bank{t}")
-            first_product(bank[:], t, slice(0, N))
-            gather(0, t - 1)
-            nc.scalar.activation(h[t][:, :N], bank[:], RELU)
-        gather(0, PACK - 1)
-        nc.scalar.activation(w2b[:], w2raw[:].rearrange("p j m -> p m j"), COPY)
-        interleave(0)
+        for t in range(3):
+            gather(t, 0, CUT)
+        for k in range(3):
+            pair(scalar_copy, k, 0)
+        for k in range(3):
+            gather(3, starts[k], starts[k] + PIECES[k])
+            pair(scalar_copy, k, 1)
         for t in range(PACK):
-            gather(1, t)
-        nc.vector.quantize_mx(out=w2q[:].bitcast(FP8X4), scales=w2s[:], in_=w2b[:].rearrange("p m j -> p (m j)"))
-        quantize_e(0)
-        second_product(0, obank[0][:])
-        interleave(1)
-        for t in range(PACK):
-            gather(2, t)
-        finish(0, obank[0][:])
-        quantize_e(1)
-        second_product(1, obank[1][:])
-        interleave(2)
-        for t in range(PACK):
-            gather(3, t)
-        finish(1, obank[1][:])
-        nc.scalar.activation(eb[3][:, :, 0:2], ef[3][:, 0:2, :].rearrange("p t n -> p n t"), COPY)
-        quantize_e(2)
-        second_product(2, obank[2][:])
-        nc.vector.tensor_copy(eb[3][:, :, 2:4], ef[3][:, 2:4, :].rearrange("p t n -> p n t"))
-        finish(2, obank[2][:])
-        quantize_e(3)
-        last = psum.tile([P, PIECES[3]], F32, name="obank3", tag="ob0")
-        second_product(3, last[:])
-        finish(3, last[:])
+            gather(t, CUT, G)
+        pair(scalar_copy, 3, 0)
+        pair(nc.vector.tensor_copy, 3, 1)
+        for k in range(4):
+            quantize_e(k)
+            second_product(k)

@@ -14,10 +14,14 @@ RELU = mybir.ActivationFunctionType.Relu
 
 P = 128
 PACK = 4
-W1_CUTS = ((0, 256), (256, 512))
-CUT = 896
-WINDOWS = (912, 912, 912, 544)
-PIECES = (512, 256, 128, 128)
+STRIPE = 16
+HALF_N = N // 2
+HALF_H = H // 2
+HALF_M = P // 2
+HALF_G = G // 2
+WINDOW = N + 32
+PARTS = (256, 256, 256, 128, 128)
+STARTS = tuple(sum(PARTS[:k]) for k in range(len(PARTS) + 1))
 
 
 def tile_attend_hop_pick_kernel(tc, xT, w1, w2, offs, offs2, out):
@@ -26,150 +30,151 @@ def tile_attend_hop_pick_kernel(tc, xT, w1, w2, offs, offs2, out):
         tc.tile_pool(name="held", bufs=1) as held,
         tc.psum_pool(name="psum", bufs=1) as psum,
     ):
-        list1 = held.tile([P, N // 16], U16, name="list1")
-        list2 = held.tile([P, G // 16], U16, name="list2")
-        xp = [held.tile([P, T], F32, name=f"xp{t}", align_bytes=64) for t in range(PACK)]
-        w1raw = [held.tile([P, PACK, hi - lo], F32, name=f"w1raw{k}", align_bytes=64) for k, (lo, hi) in enumerate(W1_CUTS)]
-        w2raw = held.tile([P, PACK, M], F32, name="w2raw", align_bytes=64)
-        xb = held.tile([P, N, PACK], BF16, name="xb", align_bytes=64)
-        xq = held.tile([P, N], U32, name="xq", align_bytes=64)
-        xs = held.tile([P, N], U8, name="xs", align_bytes=64)
-        w1b = held.tile([P, PACK, P, PACK], BF16, name="w1b", align_bytes=64)
-        w1q = held.tile([P, PACK, P], U32, name="w1q", align_bytes=64)
-        w1s = held.tile([P, PACK, P], U8, name="w1s", align_bytes=64)
-        w2b = held.tile([P, M, PACK], BF16, name="w2b", align_bytes=64)
-        w2q = held.tile([P, M], U32, name="w2q", align_bytes=64)
-        w2s = held.tile([P, M], U8, name="w2s", align_bytes=64)
-        h = [held.tile([P, w], F32, name=f"h{t}", align_bytes=64) for t, w in enumerate(WINDOWS)]
-        ef = [held.tile([P, 2, G], F32, name=f"ef{k}", align_bytes=64) for k in range(2)]
-        eb = [held.tile([P, n, PACK], BF16, name=f"eb{k}", align_bytes=64) for k, n in enumerate(PIECES)]
-        eq = [held.tile([P, n], U32, name=f"eq{k}", align_bytes=64) for k, n in enumerate(PIECES)]
-        es = [held.tile([P, n], U8, name=f"es{k}", align_bytes=64) for k, n in enumerate(PIECES)]
-        res = [held.tile([P, n], F32, name=f"res{k}", align_bytes=64) for k, n in enumerate(PIECES)]
+        idx = held.tile([P, N // STRIPE], U16)
+        idx2 = held.tile([P, G // STRIPE], U16)
+
+        x_plane = [held.tile([P, T], F32, name=f"x_plane{t}", align_bytes=64) for t in range(PACK)]
+        x_grouped = held.tile([P, N, PACK], BF16, align_bytes=64)
+        x_codes = held.tile([P, N], U32, align_bytes=64)
+        x_scales = held.tile([P, N], U8, align_bytes=64)
+
+        w1_raw = [held.tile([P, PACK, HALF_H], F32, name=f"w1_raw{k}", align_bytes=64) for k in range(2)]
+        w1_grouped = held.tile([P, PACK, P, PACK], BF16, align_bytes=64)
+        w1_codes = held.tile([P, PACK, P], U32, align_bytes=64)
+        w1_scales = held.tile([P, PACK, P], U8, align_bytes=64)
+
+        w2_raw = held.tile([P, PACK, M], F32, align_bytes=64)
+        w2_grouped = held.tile([P, M, PACK], BF16, align_bytes=64)
+        w2_codes = held.tile([P, M], U32, align_bytes=64)
+        w2_scales = held.tile([P, M], U8, align_bytes=64)
+
+        h_plane = [held.tile([P, WINDOW], F32, name=f"h_plane{t}", align_bytes=64) for t in range(PACK)]
+        e_picked = [
+            [held.tile([P, 2, HALF_G], F32, name=f"e_picked{q}{s}", align_bytes=64) for s in range(2)]
+            for q in range(2)
+        ]
+        e_grouped = held.tile([P, G, PACK], BF16, align_bytes=64)
+        e_codes = [held.tile([P, n], U32, name=f"e_codes{k}", align_bytes=64) for k, n in enumerate(PARTS)]
+        e_scales = [held.tile([P, n], U8, name=f"e_scales{k}", align_bytes=64) for k, n in enumerate(PARTS)]
+        result = held.tile([P, G], F32, align_bytes=64)
 
         x_rows = xT.rearrange("(p t) n -> p t n", t=PACK)
         w1_rows = w1.rearrange("(p j) c -> p j c", j=PACK)
-        w2_rows = w2.rearrange("(p j) m -> p j m", j=PACK)
-        nc.sync.dma_start(list1[:], offs)
-        nc.sync.dma_start(list2[:], offs2)
-        for t in range(3):
-            nc.sync.dma_start(xp[t][:], x_rows[:, t, :])
-        nc.sync.dma_start(w1raw[0][:], w1_rows[:, :, slice(*W1_CUTS[0])])
-        nc.sync.dma_start(xp[3][:], x_rows[:, 3, :])
-        nc.sync.dma_start(w1raw[1][:], w1_rows[:, :, slice(*W1_CUTS[1])])
-        nc.sync.dma_start(w2raw[:], w2_rows)
+        nc.sync.dma_start(idx[:], offs)
+        nc.sync.dma_start(idx2[:], offs2)
+        for t in range(PACK - 1):
+            nc.sync.dma_start(x_plane[t][:], x_rows[:, t, :])
+        nc.sync.dma_start(w1_raw[0][:], w1_rows[:, :, :HALF_H])
+        nc.sync.dma_start(x_plane[PACK - 1][:], x_rows[:, PACK - 1, :])
+        nc.sync.dma_start(w1_raw[1][:], w1_rows[:, :, HALF_H:])
+        nc.sync.dma_start(w2_raw[:], w2.rearrange("(p j) m -> p j m", j=PACK))
         for t in range(PACK):
-            nc.gpsimd.memset(h[t][:, N:], 0.0)
-
-        def w1_slice(k, t0, t1):
-            lo, hi = W1_CUTS[k]
-            m0, m1 = lo // PACK, hi // PACK
-            src = w1raw[k][:].rearrange("p j (m t) -> p m t j", t=PACK)
-            dst = w1b[:].rearrange("p t m j -> p m t j")
-            nc.scalar.activation(dst[:, m0:m1, t0:t1, :], src[:, :, t0:t1, :], COPY)
-
-        def quantize_w1(t):
-            nc.vector.quantize_mx(
-                out=w1q[:, t, :].bitcast(FP8X4),
-                scales=w1s[:, t, :],
-                in_=w1b[:, t, :, :].rearrange("p m j -> p (m j)"),
-            )
-
-        for t in range(3):
-            nc.vector.tensor_copy(xb[:, :, t], xp[t][:].indirect(list1[:]))
-        w1_slice(0, 0, PACK)
-        half = N // 2
-        for a in range(2):
-            nc.vector.tensor_copy(
-                xb[:, a * half : (a + 1) * half, 3],
-                xp[3][:].indirect(list1[:, a * half // 16 : (a + 1) * half // 16]),
-            )
-
-        w1_slice(1, 0, 1)
-        w1_slice(1, 1, PACK)
-
-        def quantize_x(a):
-            cols = slice(a * half, (a + 1) * half)
-            nc.vector.quantize_mx(
-                out=xq[:, cols].bitcast(FP8X4),
-                scales=xs[:, cols],
-                in_=xb[:, cols, :].rearrange("p n j -> p (n j)"),
-            )
-
-        def first_product(bank, t, cols):
-            nc.tensor.matmul_mx(
-                out=bank,
-                lhsT=w1q[:, t, :].bitcast(FP8X4),
-                lhsT_scale=w1s[:, t, :],
-                rhs=xq[:, cols].bitcast(FP8X4),
-                rhs_scale=xs[:, cols],
-                start=True,
-                stop=True,
-            )
-
-        quantize_x(0)
-        quantize_w1(0)
-        quantize_x(1)
-        bank0 = [psum.tile([P, half], F32, name=f"bank0{a}") for a in range(2)]
-        for a in range(2):
-            first_product(bank0[a][:], 0, slice(a * half, (a + 1) * half))
-        nc.scalar.activation(h[0][:, :half], bank0[0][:], RELU)
-        nc.vector.tensor_relu(h[0][:, half:N], bank0[1][:])
-        for t in range(1, PACK):
-            quantize_w1(t)
-            bank = psum.tile([P, N], F32, name=f"bank{t}")
-            first_product(bank[:], t, slice(0, N))
-            nc.scalar.activation(h[t][:, :N], bank[:], RELU)
-        nc.scalar.activation(w2b[:], w2raw[:].rearrange("p j m -> p m j"), COPY)
-        nc.vector.quantize_mx(out=w2q[:].bitcast(FP8X4), scales=w2s[:], in_=w2b[:].rearrange("p m j -> p (m j)"))
-
-        starts = [sum(PIECES[:k]) for k in range(len(PIECES))]
-
-        def gather(t, lo, hi):
-            nc.vector.tensor_copy(ef[t // 2][:, t % 2, lo:hi], h[t][:].indirect(list2[:, lo // 16 : hi // 16]))
-
-        def pair(engine_copy, k, half_word):
-            cols = slice(starts[k], starts[k] + PIECES[k])
-            engine_copy(
-                eb[k][:, :, 2 * half_word : 2 * half_word + 2],
-                ef[half_word][:, :, cols].rearrange("p t n -> p n t"),
-            )
+            nc.gpsimd.memset(h_plane[t][:, N:], 0.0)
 
         def scalar_copy(dst, src):
             nc.scalar.activation(dst, src, COPY)
 
-        def quantize_e(k):
+        def quantize(codes, scales, grouped):
             nc.vector.quantize_mx(
-                out=eq[k][:].bitcast(FP8X4),
-                scales=es[k][:],
-                in_=eb[k][:].rearrange("p n j -> p (n j)"),
+                out=codes.bitcast(FP8X4),
+                scales=scales,
+                in_=grouped.rearrange("p c j -> p (c j)"),
             )
 
-        def second_product(k):
-            bank = psum.tile([P, PIECES[k]], F32, name=f"obank{k}", tag="bank00" if k == 3 else f"ob{k}")
+        def multiply(bank, left_codes, left_scales, right_codes, right_scales):
             nc.tensor.matmul_mx(
-                out=bank[:],
-                lhsT=w2q[:].bitcast(FP8X4),
-                lhsT_scale=w2s[:],
-                rhs=eq[k][:].bitcast(FP8X4),
-                rhs_scale=es[k][:],
+                out=bank,
+                lhsT=left_codes.bitcast(FP8X4),
+                lhsT_scale=left_scales,
+                rhs=right_codes.bitcast(FP8X4),
+                rhs_scale=right_scales,
                 start=True,
                 stop=True,
             )
-            (nc.vector.tensor_copy if k > 2 else nc.scalar.copy)(res[k][:], bank[:])
-            nc.sync.dma_start(out[:, starts[k] : starts[k] + PIECES[k]], res[k][:])
 
-        for t in range(3):
-            gather(t, 0, CUT)
-        for k in range(3):
-            pair(scalar_copy, k, 0)
-        for k in range(3):
-            gather(3, starts[k], starts[k] + PIECES[k])
-            pair(scalar_copy, k, 1)
+        def group_w1(k, t0, t1):
+            ms = slice(k * HALF_M, (k + 1) * HALF_M)
+            scalar_copy(
+                w1_grouped[:].rearrange("p t m j -> p m t j")[:, ms, t0:t1, :],
+                w1_raw[k][:].rearrange("p j (m t) -> p m t j", t=PACK)[:, :, t0:t1, :],
+            )
+
+        def quantize_w1(t, k):
+            ms = slice(k * HALF_M, (k + 1) * HALF_M)
+            quantize(w1_codes[:, t, ms], w1_scales[:, t, ms], w1_grouped[:, t, ms, :])
+
+        for t in range(PACK - 1):
+            nc.vector.tensor_copy(x_grouped[:, :, t], x_plane[t][:].indirect(idx[:]))
+        group_w1(0, 0, PACK)
         for t in range(PACK):
-            gather(t, CUT, G)
-        pair(scalar_copy, 3, 0)
-        pair(nc.vector.tensor_copy, 3, 1)
-        for k in range(4):
-            quantize_e(k)
-            second_product(k)
+            quantize_w1(t, 0)
+        n_halves = [slice(a * HALF_N, (a + 1) * HALF_N) for a in range(2)]
+        for cols in n_halves:
+            entries = idx[:, cols.start // STRIPE : cols.stop // STRIPE]
+            nc.vector.tensor_copy(x_grouped[:, cols, PACK - 1], x_plane[PACK - 1][:].indirect(entries))
+        group_w1(1, 0, 1)
+        group_w1(1, 1, PACK)
+
+        def quantize_x(cols):
+            quantize(x_codes[:, cols], x_scales[:, cols], x_grouped[:, cols, :])
+
+        def first_product(bank, t, cols):
+            multiply(bank, w1_codes[:, t, :], w1_scales[:, t, :], x_codes[:, cols], x_scales[:, cols])
+
+        quantize_x(n_halves[0])
+        quantize_w1(0, 1)
+        quantize_x(n_halves[1])
+        bank_halves = [psum.tile([P, HALF_N], F32, name=f"bank_half{a}") for a in range(2)]
+        for bank, cols in zip(bank_halves, n_halves):
+            first_product(bank[:], 0, cols)
+        nc.scalar.activation(h_plane[0][:, n_halves[0]], bank_halves[0][:], RELU)
+        for t in range(1, PACK):
+            quantize_w1(t, 1)
+        nc.vector.tensor_relu(h_plane[0][:, n_halves[1]], bank_halves[1][:])
+        for t in range(1, PACK):
+            bank = psum.tile([P, N], F32, name=f"bank{t}")
+            first_product(bank[:], t, slice(0, N))
+            nc.scalar.activation(h_plane[t][:, :N], bank[:], RELU)
+
+        scalar_copy(w2_grouped[:], w2_raw[:].rearrange("p j m -> p m j"))
+        quantize(w2_codes[:], w2_scales[:], w2_grouped[:])
+
+        def pick(t, lo, hi):
+            s = lo // HALF_G
+            nc.vector.tensor_copy(
+                e_picked[t // 2][s][:, t % 2, lo - s * HALF_G : hi - s * HALF_G],
+                h_plane[t][:].indirect(idx2[:, lo // STRIPE : hi // STRIPE]),
+            )
+
+        def group_e(q, lo, hi):
+            s = lo // HALF_G
+            scalar_copy(
+                e_grouped[:, lo:hi, 2 * q : 2 * q + 2],
+                e_picked[q][s][:, :, lo - s * HALF_G : hi - s * HALF_G].rearrange("p u c -> p c u"),
+            )
+
+        def finish(first, last, empty_bank):
+            lo, hi = STARTS[first], STARTS[last + 1]
+            bank = psum.tile([P, hi - lo], F32, name=f"bank_out{first}")
+            for k in range(first, last + 1):
+                quantize(e_codes[k][:], e_scales[k][:], e_grouped[:, STARTS[k] : STARTS[k + 1], :])
+                columns = bank[:, STARTS[k] - lo : STARTS[k + 1] - lo]
+                multiply(columns, w2_codes[:], w2_scales[:], e_codes[k][:], e_scales[k][:])
+            empty_bank(result[:, lo:hi], bank[:])
+            nc.sync.dma_start(out[:, lo:hi], result[:, lo:hi])
+
+        for s in range(2):
+            for t in range(2):
+                pick(t, s * HALF_G, (s + 1) * HALF_G)
+            group_e(0, s * HALF_G, (s + 1) * HALF_G)
+        for t in range(2, PACK):
+            pick(t, 0, HALF_G)
+        for k in range(2):
+            group_e(1, STARTS[k], STARTS[k + 1])
+        pick(2, HALF_G, G)
+        for k in range(2, len(PARTS)):
+            pick(3, STARTS[k], STARTS[k + 1])
+            group_e(1, STARTS[k], STARTS[k + 1])
+        finish(0, 1, nc.scalar.copy)
+        finish(2, 2, nc.scalar.copy)
+        finish(3, 4, nc.vector.tensor_copy)

import concourse.mybir as mybir

D, T, N, H, M, G = 512, 2048, 512, 512, 128, 1024
FLOPS = 2 * D * H * N + 2 * H * M * G

F32 = mybir.dt.float32
BF16 = mybir.dt.bfloat16
U32 = mybir.dt.uint32
U16 = mybir.dt.uint16
U8 = mybir.dt.uint8
FP8X4 = mybir.dt.float8_e4m3fn_x4
COPY = mybir.ActivationFunctionType.Copy
RELU = mybir.ActivationFunctionType.Relu

P = 128
PACK = 4
STRIPE = 16
HALF_N = N // 2
HALF_H = H // 2
HALF_M = P // 2
HALF_G = G // 2
WINDOW = N + 32
PARTS = (256, 256, 256, 128, 128)
STARTS = tuple(sum(PARTS[:k]) for k in range(len(PARTS) + 1))


def tile_attend_hop_pick_kernel(tc, xT, w1, w2, offs, offs2, out):
    nc = tc.nc
    with (
        tc.tile_pool(name="held", bufs=1) as held,
        tc.psum_pool(name="psum", bufs=1) as psum,
    ):
        idx = held.tile([P, N // STRIPE], U16)
        idx2 = held.tile([P, G // STRIPE], U16)

        x_plane = [held.tile([P, T], F32, name=f"x_plane{t}", align_bytes=64) for t in range(PACK)]
        x_grouped = held.tile([P, N, PACK], BF16, align_bytes=64)
        x_codes = held.tile([P, N], U32, align_bytes=64)
        x_scales = held.tile([P, N], U8, align_bytes=64)

        w1_raw = [held.tile([P, PACK, HALF_H], F32, name=f"w1_raw{k}", align_bytes=64) for k in range(2)]
        w1_grouped = held.tile([P, PACK, P, PACK], BF16, align_bytes=64)
        w1_codes = held.tile([P, PACK, P], U32, align_bytes=64)
        w1_scales = held.tile([P, PACK, P], U8, align_bytes=64)

        w2_raw = held.tile([P, PACK, M], F32, align_bytes=64)
        w2_grouped = held.tile([P, M, PACK], BF16, align_bytes=64)
        w2_codes = held.tile([P, M], U32, align_bytes=64)
        w2_scales = held.tile([P, M], U8, align_bytes=64)

        h_plane = [held.tile([P, WINDOW], F32, name=f"h_plane{t}", align_bytes=64) for t in range(PACK)]
        e_picked = [
            [held.tile([P, 2, HALF_G], F32, name=f"e_picked{q}{s}", align_bytes=64) for s in range(2)]
            for q in range(2)
        ]
        e_grouped = held.tile([P, G, PACK], BF16, align_bytes=64)
        e_codes = [held.tile([P, n], U32, name=f"e_codes{k}", align_bytes=64) for k, n in enumerate(PARTS)]
        e_scales = [held.tile([P, n], U8, name=f"e_scales{k}", align_bytes=64) for k, n in enumerate(PARTS)]
        result = held.tile([P, G], F32, align_bytes=64)

        x_rows = xT.rearrange("(p t) n -> p t n", t=PACK)
        w1_rows = w1.rearrange("(p j) c -> p j c", j=PACK)
        nc.sync.dma_start(idx[:], offs)
        nc.sync.dma_start(idx2[:], offs2)
        for t in range(PACK - 1):
            nc.sync.dma_start(x_plane[t][:], x_rows[:, t, :])
        nc.sync.dma_start(w1_raw[0][:], w1_rows[:, :, :HALF_H])
        nc.sync.dma_start(x_plane[PACK - 1][:], x_rows[:, PACK - 1, :])
        nc.sync.dma_start(w1_raw[1][:], w1_rows[:, :, HALF_H:])
        nc.sync.dma_start(w2_raw[:], w2.rearrange("(p j) m -> p j m", j=PACK))
        for t in range(PACK):
            nc.gpsimd.memset(h_plane[t][:, N:], 0.0)

        def scalar_copy(dst, src):
            nc.scalar.activation(dst, src, COPY)

        def quantize(codes, scales, grouped):
            nc.vector.quantize_mx(
                out=codes.bitcast(FP8X4),
                scales=scales,
                in_=grouped.rearrange("p c j -> p (c j)"),
            )

        def multiply(bank, left_codes, left_scales, right_codes, right_scales):
            nc.tensor.matmul_mx(
                out=bank,
                lhsT=left_codes.bitcast(FP8X4),
                lhsT_scale=left_scales,
                rhs=right_codes.bitcast(FP8X4),
                rhs_scale=right_scales,
                start=True,
                stop=True,
            )

        def group_w1(k, t0, t1):
            ms = slice(k * HALF_M, (k + 1) * HALF_M)
            scalar_copy(
                w1_grouped[:].rearrange("p t m j -> p m t j")[:, ms, t0:t1, :],
                w1_raw[k][:].rearrange("p j (m t) -> p m t j", t=PACK)[:, :, t0:t1, :],
            )

        def quantize_w1(t, k):
            ms = slice(k * HALF_M, (k + 1) * HALF_M)
            quantize(w1_codes[:, t, ms], w1_scales[:, t, ms], w1_grouped[:, t, ms, :])

        for t in range(PACK - 1):
            nc.vector.tensor_copy(x_grouped[:, :, t], x_plane[t][:].indirect(idx[:]))
        group_w1(0, 0, PACK)
        for t in range(PACK):
            quantize_w1(t, 0)
        n_halves = [slice(a * HALF_N, (a + 1) * HALF_N) for a in range(2)]
        for cols in n_halves:
            entries = idx[:, cols.start // STRIPE : cols.stop // STRIPE]
            nc.vector.tensor_copy(x_grouped[:, cols, PACK - 1], x_plane[PACK - 1][:].indirect(entries))
        group_w1(1, 0, 1)
        group_w1(1, 1, PACK)

        def quantize_x(cols):
            quantize(x_codes[:, cols], x_scales[:, cols], x_grouped[:, cols, :])

        def first_product(bank, t, cols):
            multiply(bank, w1_codes[:, t, :], w1_scales[:, t, :], x_codes[:, cols], x_scales[:, cols])

        quantize_x(n_halves[0])
        quantize_w1(0, 1)
        quantize_x(n_halves[1])
        bank_halves = [psum.tile([P, HALF_N], F32, name=f"bank_half{a}") for a in range(2)]
        for bank, cols in zip(bank_halves, n_halves):
            first_product(bank[:], 0, cols)
        nc.scalar.activation(h_plane[0][:, n_halves[0]], bank_halves[0][:], RELU)
        for t in range(1, PACK):
            quantize_w1(t, 1)
        nc.vector.tensor_relu(h_plane[0][:, n_halves[1]], bank_halves[1][:])
        for t in range(1, PACK):
            bank = psum.tile([P, N], F32, name=f"bank{t}")
            first_product(bank[:], t, slice(0, N))
            nc.scalar.activation(h_plane[t][:, :N], bank[:], RELU)

        scalar_copy(w2_grouped[:], w2_raw[:].rearrange("p j m -> p m j"))
        quantize(w2_codes[:], w2_scales[:], w2_grouped[:])

        def pick(t, lo, hi):
            s = lo // HALF_G
            nc.vector.tensor_copy(
                e_picked[t // 2][s][:, t % 2, lo - s * HALF_G : hi - s * HALF_G],
                h_plane[t][:].indirect(idx2[:, lo // STRIPE : hi // STRIPE]),
            )

        def group_e(q, lo, hi):
            s = lo // HALF_G
            scalar_copy(
                e_grouped[:, lo:hi, 2 * q : 2 * q + 2],
                e_picked[q][s][:, :, lo - s * HALF_G : hi - s * HALF_G].rearrange("p u c -> p c u"),
            )

        def finish(first, last, empty_bank):
            lo, hi = STARTS[first], STARTS[last + 1]
            bank = psum.tile([P, hi - lo], F32, name=f"bank_out{first}")
            for k in range(first, last + 1):
                quantize(e_codes[k][:], e_scales[k][:], e_grouped[:, STARTS[k] : STARTS[k + 1], :])
                columns = bank[:, STARTS[k] - lo : STARTS[k + 1] - lo]
                multiply(columns, w2_codes[:], w2_scales[:], e_codes[k][:], e_scales[k][:])
            empty_bank(result[:, lo:hi], bank[:])
            nc.sync.dma_start(out[:, lo:hi], result[:, lo:hi])

        for s in range(2):
            for t in range(2):
                pick(t, s * HALF_G, (s + 1) * HALF_G)
            group_e(0, s * HALF_G, (s + 1) * HALF_G)
        for t in range(2, PACK):
            pick(t, 0, HALF_G)
        for k in range(2):
            group_e(1, STARTS[k], STARTS[k + 1])
        pick(2, HALF_G, G)
        for k in range(2, len(PARTS)):
            pick(3, STARTS[k], STARTS[k + 1])
            group_e(1, STARTS[k], STARTS[k + 1])
        finish(0, 1, nc.scalar.copy)
        finish(2, 2, nc.scalar.copy)
        finish(3, 4, nc.vector.tensor_copy)
